import numpy as np
import ml_dtypes


def mxq(x, axis, fmt="e4m3"):
    dtype, down = {"e4m3": (ml_dtypes.float8_e4m3fn, 7), "e5m2": (ml_dtypes.float8_e5m2, 14)}[fmt]
    v = np.moveaxis(np.asarray(x, np.float32).astype(ml_dtypes.bfloat16).astype(np.float64), axis, -1)
    blocks = v.reshape(v.shape[:-1] + (-1, 32))
    amax = np.abs(blocks).max(-1, keepdims=True)
    byte = np.maximum(np.where(amax > 0, np.frexp(amax)[1] - 1 + 127, 0) - down, 1)
    scale = np.exp2(byte - 127.0)
    codes = (blocks / scale).astype(np.float32).astype(dtype).astype(np.float64)
    return np.moveaxis((codes * scale).reshape(v.shape), -1, axis)


WIDE = False


def mx_kscale(k):
    if not WIDE:
        return np.ones(k)
    levels = np.array([10, -10, 5, -5, 0])
    if k % 512:
        return np.exp2(np.random.permutation(np.resize(levels, k // 32))).repeat(32)
    a = np.empty((k // 512, 16))
    for p in range(k // 512):
        a[p, :8] = np.random.permutation(np.resize(levels, 8))
        for g in range(8):
            far = levels[np.abs(levels - a[p, g]) >= 10]
            a[p, g + 8] = far[np.random.randint(len(far))]
    return np.exp2(a.ravel()).repeat(32)


def f64(x):
    return np.asarray(x).astype(np.float64)


def striped(idx):
    return np.tile(idx.reshape(-1, 16).T, (8, 1)).astype(np.uint16)


def unstriped(offs):
    return offs[:16].T.reshape(-1).astype(np.int64)


def pack_weight(w):
    k, n = w.shape
    w = f64(np.asarray(w, np.float32).astype(ml_dtypes.bfloat16)).reshape(k // 32, 32, n)
    amax = np.abs(w).max(1)
    byte = np.clip(np.where(amax > 0, np.frexp(amax)[1] - 1 + 127 - 7, 1), 1, 254)
    scaled = (w * np.exp2(127.0 - byte)[:, None, :]).reshape(k, n).astype(np.float32)
    words = np.ascontiguousarray(scaled.reshape(k // 512, 128, 4, n).transpose(0, 1, 3, 2)).astype(ml_dtypes.float8_e4m3fn).view(np.uint8)
    return words, np.ascontiguousarray(byte.astype(np.uint8).reshape(k // 512, 16, n))


def unpack_weight(words, scales):
    g, p, n, _ = words.shape
    vals = np.ascontiguousarray(words).view(ml_dtypes.float8_e4m3fn).astype(np.float64) * np.repeat(np.exp2(scales.astype(np.float64) - 127.0), 8, axis=1)[..., None]
    return vals.transpose(0, 1, 3, 2).reshape(g * 512, n)


def sigmoid(v):
    return 1.0 / (1.0 + np.exp(-np.maximum(v, -700.0)))


K, T, S, N = 1024, 1024, 512, 256
P = 2 ** 7


def setup_inputs():
    n = np.random.standard_normal
    s = mx_kscale(K)[:, None]
    packed_xT = pack_weight(n((K, T)) * s)
    return {
        "x_words": packed_xT[0],
        "x_scales": packed_xT[1],
        "w1": (n((K, N)) / np.sqrt(K) / s).astype(np.float32),
        "w2": (n((K, N)) / np.sqrt(K) / s).astype(np.float32),
        "rser": (np.tile(np.random.uniform(0.05, 0.3, S), (P, 1))).astype(np.float32),
        "isat": (np.random.uniform(0.05, 0.2, (N, 1))).astype(np.float32),
        "gsh": (np.tile(np.random.uniform(0.02, 0.2, S), (P, 1))).astype(np.float32),
        "offs": striped(np.random.permutation(T)[:S]),
        "mate": striped(np.random.permutation(S)),
    }


def reference(x_words, x_scales, w1, w2, rser, isat, gsh, offs, mate):
    xq = unpack_weight(x_words, x_scales)[:, unstriped(offs)]
    yi = mxq(f64(w1), 0, "e4m3").T @ xq
    ilit = np.log(np.exp(yi) + 1.0) + 0.3
    yv = mxq(f64(w2), 0, "e4m3").T @ xq
    volt = 1.5 * sigmoid(yv)
    vda = volt + ilit * f64(rser)[:1]
    exa = f64(isat) * np.exp(1.3 * vda)
    rsa = ilit - exa - (f64(gsh)[:1] * vda) - ilit
    cua = ilit + rsa / (f64(rser)[:1] * (1.3 * exa + f64(gsh)[:1]) + 1.0)
    return (np.minimum(cua, cua[:, unstriped(mate)])) * (volt + volt[:, unstriped(mate)])

@@ -1,0 +1,256 @@
+from contextlib import ExitStack
+
+import concourse.mybir as mybir
+from concourse.masks import make_identity
+
+K, T, S, N = 1024, 1024, 512, 256
+FLOPS = 2 * 2 * K * N * S
+
+F32 = mybir.dt.float32
+BF16 = mybir.dt.bfloat16
+U32 = mybir.dt.uint32
+I32 = mybir.dt.int32
+U16 = mybir.dt.uint16
+U8 = mybir.dt.uint8
+FP8X4 = mybir.dt.float8_e4m3fn_x4
+ALU = mybir.AluOpType
+ACT = mybir.ActivationFunctionType
+
+P = 128
+PACK = 4
+PASSES = K // (P * PACK)
+JB = S // P
+HALVES = N // P
+PIECE = 256
+LN_TOP = 2.0 ** 60
+LN_FLOOR = 2.0 ** -60
+
+
+def tile_picked_ypvcel_pow_p_kernel(
+    tc, x_words, x_scales, w1, w2, rser, isat, gsh, offs, mate, out
+):
+    nc = tc.nc
+    with ExitStack() as ctx:
+        keep = ctx.enter_context(tc.tile_pool(name="keep", bufs=1))
+        psum = ctx.enter_context(tc.psum_pool(name="psum", bufs=1))
+
+        def sb(name, width, dtype=F32):
+            return keep.tile([P, width], dtype, name=name, align_bytes=64)
+
+        def bank(name, tag):
+            return psum.tile([P, S], F32, name=name, tag=tag)
+
+        def blk(b):
+            return slice(b * P, (b + 1) * P)
+
+        offs_t = keep.tile([P, S // 16], U16, name="offs_t")
+        mate_t = keep.tile([P, S // 16], U16, name="mate_t")
+        word_win = [sb("word_win%d" % g, T, U32) for g in range(PASSES)]
+        scale_win = sb("scale_win", T, U8)
+        raw = {(w, g): sb("raw%d_%d" % (w, g), PACK * N) for w in (1, 2) for g in range(PASSES)}
+        rows = sb("rows", P)
+        ident = sb("ident", P)
+
+        def load_words(g):
+            nc.sync.dma_start(
+                out=word_win[g][:].bitcast(I32),
+                in_=x_words[g].rearrange("p n t -> p (n t)").bitcast(I32),
+            )
+
+        def load_weight(w, g):
+            src = (w1 if w == 1 else w2)[g * P * PACK : (g + 1) * P * PACK, :]
+            nc.sync.dma_start(out=raw[w, g][:], in_=src.rearrange("(p j) c -> p (j c)", j=PACK))
+
+        nc.vector.memset(scale_win[:].bitcast(I32), 0)
+        nc.gpsimd.memset(rows[:], 0.0)
+        nc.sync.dma_start(offs_t[:], offs)
+        load_words(0)
+        for q in range(4):
+            nc.sync.dma_start(
+                out=scale_win[32 * q : 32 * q + 4 * PASSES, :].bitcast(I32),
+                in_=x_scales[:, 4 * q : 4 * q + 4, :].bitcast(I32),
+            )
+        load_weight(2, 0)
+        load_words(1)
+        nc.sync.dma_start(out=rows[0:JB, :], in_=rser[0:1, :].rearrange("o (b p) -> (o b) p", p=P))
+        nc.sync.dma_start(out=rows[JB : 2 * JB, :], in_=gsh[0:1, :].rearrange("o (b p) -> (o b) p", p=P))
+        nc.sync.dma_start(out=rows[2 * JB : 2 * JB + HALVES, :], in_=isat.rearrange("(h p) o -> (o h) p", p=P))
+        load_weight(2, 1)
+        load_weight(1, 0)
+        load_weight(1, 1)
+        nc.sync.dma_start(mate_t[:], mate)
+        make_identity(nc, ident[:])
+
+        turned = bank("turned", "d0")
+        nc.tensor.transpose(turned[:, 0:P], rows[:], ident[:])
+        par = sb("par", 16)
+        nc.scalar.activation(par[:, 0:10], turned[:, 0:10], ACT.Copy)
+        r_c, g_c, isat_c = par[:, 0:JB], par[:, JB : 2 * JB], par[:, 2 * JB : 2 * JB + HALVES]
+        expo = sb("expo", HALVES * S + 8)
+        ac = sb("ac", 2 * JB)
+        rg = sb("rg", JB)
+        nc.gpsimd.tensor_scalar(ac[:, 0:JB], r_c, 1.3, LN_FLOOR, ALU.mult, ALU.max)
+        nc.gpsimd.tensor_tensor(rg[:], r_c, g_c, ALU.mult)
+        nc.gpsimd.tensor_scalar(ac[:, JB : 2 * JB], rg[:], 1.0, 1.0, ALU.mult, ALU.add)
+        inv = sb("inv", 2 * JB)
+        nc.vector.reciprocal(inv[:], ac[:])
+        inv_a, inv_c = inv[:, 0:JB], inv[:, JB : 2 * JB]
+        nc.gpsimd.tensor_tensor(expo[:, HALVES * S : HALVES * S + JB], ac[:, 0:JB], inv_c, ALU.mult)
+        nc.gpsimd.tensor_scalar(expo[:, HALVES * S + JB : HALVES * S + JB + HALVES], isat_c, 1.0, LN_FLOOR, ALU.mult, ALU.max)
+        ngc = sb("ngc", JB)
+        slope = sb("slope", JB)
+        level = sb("level", JB)
+        vk = sb("vk", JB)
+        r43 = sb("r43", JB)
+        kb = sb("kb", JB)
+        nc.gpsimd.tensor_tensor(ngc[:], g_c, inv_c, ALU.mult)
+        nc.gpsimd.tensor_scalar(slope[:], ngc[:], -0.75, 0.0, ALU.mult, ALU.add)
+        nc.gpsimd.tensor_scalar(vk[:], r_c, -0.3, -0.75, ALU.mult, ALU.add)
+        nc.gpsimd.tensor_tensor(level[:], ngc[:], vk[:], ALU.mult)
+        nc.gpsimd.tensor_scalar(r43[:], r_c, 1.0 / 0.75, 0.0, ALU.mult, ALU.add)
+        nc.gpsimd.tensor_scalar(kb[:], r_c, 0.4, 1.0, ALU.mult, ALU.add)
+
+        words = [sb("words%d" % g, S, U32) for g in range(PASSES)]
+        scales = sb("scales", S, U8)
+        nc.vector.tensor_copy(words[0][:], word_win[0][:].indirect(offs_t[:]))
+        nc.vector.tensor_copy(scales[:], scale_win[:].indirect(offs_t[:]))
+        nc.vector.tensor_copy(words[1][:], word_win[1][:].indirect(offs_t[:]))
+
+        grouped = {}
+        wq = {}
+        ws = {}
+
+        def cast(w, g, h0, nh, copy):
+            t = sb("grouped%d_%d_%d" % (w, g, h0), nh * P * PACK, BF16)
+            grouped[w, g, h0] = t
+            src = raw[w, g][:].rearrange("p (j c) -> p c j", j=PACK)[:, h0 * P : (h0 + nh) * P, :]
+            copy(t[:].rearrange("p (c j) -> p c j", j=PACK), src)
+
+        def quantize(w, g, h0, nh):
+            codes = sb("wq%d_%d_%d" % (w, g, h0), nh * P, U32)
+            plane = sb("ws%d_%d_%d" % (w, g, h0), nh * P, U8)
+            nc.vector.quantize_mx(codes[:].bitcast(FP8X4), plane[:], grouped[w, g, h0][:])
+            for h in range(nh):
+                wq[w, g, h0 + h] = codes[:, blk(h)]
+                ws[w, g, h0 + h] = plane[:, blk(h)]
+
+        y = {(w, h): bank("y%d_%d" % (w, h), ("a%d" if w == 2 else "b%d") % h) for w in (1, 2) for h in range(HALVES)}
+
+        def product(w, g, h):
+            for b in range(JB):
+                nc.tensor.matmul_mx(
+                    out=y[w, h][:, blk(b)],
+                    lhsT=words[g][:, blk(b)].bitcast(FP8X4),
+                    lhsT_scale=scales[4 * g : P, blk(b)],
+                    rhs=wq[w, g, h].bitcast(FP8X4),
+                    rhs_scale=ws[w, g, h],
+                    start=(g == 0 and b == 0),
+                    stop=(g == PASSES - 1 and b == JB - 1),
+                )
+
+        for g in range(PASSES):
+            cast(2, g, 0, HALVES, lambda o, i: nc.scalar.activation(o, i, ACT.Copy))
+            quantize(2, g, 0, HALVES)
+            for h in range(HALVES):
+                product(2, g, h)
+        cast(1, 0, 0, HALVES, nc.vector.tensor_copy)
+        quantize(1, 0, 0, HALVES)
+        for h in range(HALVES):
+            product(1, 0, h)
+        for h in range(HALVES):
+            cast(1, 1, h, 1, nc.vector.tensor_copy)
+        for h in range(HALVES):
+            quantize(1, 1, h, 1)
+            product(1, 1, h)
+
+        def turn(dst, src, first, last):
+            for b in range(JB):
+                nc.tensor.matmul(
+                    dst[:, blk(b)], src(b), ident[:], start=(first and b == 0), stop=(last and b == JB - 1), is_transpose=True
+                )
+
+        def blocks(t):
+            return lambda b: t[:, blk(b)]
+
+        def spread(col):
+            return lambda b: col[:, b : b + 1].to_broadcast([P, P])
+
+        th = [sb("th%d" % h, S) for h in range(HALVES)]
+        for h in range(HALVES):
+            nc.scalar.activation(th[h][:], y[2, h][:], ACT.Tanh, scale=0.5)
+        for h in range(HALVES):
+            nc.scalar.activation(expo[:, h * S : (h + 1) * S], y[1, h][:], ACT.Exp)
+        capped = sb("capped", HALVES * S + 8)
+        n_ln = HALVES * S + JB + HALVES
+        nc.vector.tensor_scalar(capped[:, 0:n_ln], expo[:, 0:n_ln], LN_TOP, None, ALU.min)
+
+        vsum = []
+        for h in range(HALVES):
+            th_t = bank("th_t%d" % h, "c%d" % h)
+            turn(th_t, blocks(th[h]), True, True)
+            volt = sb("volt%d" % h, S)
+            volt2 = sb("volt2_%d" % h, S)
+            nc.vector.tensor_scalar(volt[:], th_t[:], 0.75, 0.75, ALU.mult, ALU.add)
+            nc.vector.tensor_copy(volt2[:], volt[:])
+            vs = sb("vsum%d" % h, S)
+            for c0 in range(0, S, PIECE):
+                nc.vector.tensor_tensor(
+                    vs[:, c0 : c0 + PIECE],
+                    volt[:].indirect(mate_t[:, c0 // 16 : (c0 + PIECE) // 16]),
+                    volt2[:, c0 : c0 + PIECE],
+                    ALU.add,
+                )
+            vsum.append(vs)
+
+        logs = sb("logs", 8)
+        nc.scalar.activation(logs[:, 0 : JB + HALVES], capped[:, HALVES * S : n_ln], ACT.Ln)
+        shift = sb("shift", JB)
+        nc.vector.scalar_tensor_tensor(shift[:], logs[:, 0:JB], 1.0 / 0.975, kb[:], ALU.mult, ALU.add)
+        soft_raw = [sb("soft_raw%d" % h, S) for h in range(HALVES)]
+        for h in range(HALVES):
+            nc.scalar.activation(soft_raw[h][:], capped[:, h * S : (h + 1) * S], ACT.Ln, bias=1.0)
+
+        u_t, w_t, x_t = [], [], []
+        for h in range(HALVES):
+            u_t.append(bank("u_t%d" % h, "a%d" % h))
+            w_t.append(bank("w_t%d" % h, "d%d" % h))
+            x_t.append(bank("x_t%d" % h, "c%d" % h))
+            turn(w_t[h], spread(inv_a), True, False)
+            turn(u_t[h], spread(shift), True, False)
+        for h in range(HALVES):
+            soft = sb("soft%d" % h, S)
+            u = sb("u%d" % h, S)
+            ngv = sb("ngv%d" % h, S)
+            nc.vector.tensor_tensor(soft[:], soft_raw[h][:], y[1, h][:], ALU.max)
+            for b in range(JB):
+                nc.vector.scalar_tensor_tensor(
+                    u[:, blk(b)], soft[:, blk(b)], r43[:, b : b + 1], th[h][:, blk(b)], ALU.mult, ALU.add
+                )
+            turn(u_t[h], blocks(u), False, True)
+            for b in range(JB):
+                nc.vector.tensor_scalar(
+                    ngv[:, blk(b)], u[:, blk(b)], slope[:, b : b + 1], level[:, b : b + 1], ALU.mult, ALU.add
+                )
+            turn(w_t[h], blocks(ngv), False, True)
+            turn(x_t[h], blocks(soft), True, False)
+            turn(x_t[h], blocks(ngv), False, True)
+
+        cua = []
+        for h in range(HALVES):
+            gate = sb("gate%d" % h, S)
+            nc.scalar.activation(gate[:], u_t[h][:], ACT.Sigmoid, bias=logs[:, JB + h : JB + h + 1], scale=0.975)
+            pull = sb("pull%d" % h, S)
+            nc.vector.tensor_tensor(pull[:], gate[:], w_t[h][:], ALU.mult)
+            c = sb("cua%d" % h, S)
+            nc.vector.scalar_tensor_tensor(c[:], x_t[h][:], 0.3, pull[:], ALU.add, ALU.subtract)
+            cua.append(c)
+        for h in range(HALVES):
+            for c0 in range(0, S, PIECE):
+                cols = slice(c0, c0 + PIECE)
+                other = sb("other%d_%d" % (h, c0), PIECE)
+                nc.scalar.activation(other[:], cua[h][:].indirect(mate_t[:, c0 // 16 : (c0 + PIECE) // 16]), ACT.Copy)
+                least = sb("least%d_%d" % (h, c0), PIECE)
+                nc.vector.tensor_tensor(least[:], other[:], cua[h][:, cols], ALU.min)
+                res = sb("res%d_%d" % (h, c0), PIECE)
+                nc.vector.tensor_tensor(res[:], least[:], vsum[h][:, cols], ALU.mult)
+                nc.sync.dma_start(out=out[blk(h), cols], in_=res[:])

@@ -22,8 +22,9 @@ PASSES = K // (P * PACK)
 JB = S // P
 HALVES = N // P
 PIECE = 256
-LN_TOP = 2.0 ** 60
 LN_FLOOR = 2.0 ** -60
+A_FLOOR = 2.0 ** -50
+LAP = 16
 
 
 def tile_picked_ypvcel_pow_p_kernel(
@@ -34,8 +35,8 @@ def tile_picked_ypvcel_pow_p_kernel(
         keep = ctx.enter_context(tc.tile_pool(name="keep", bufs=1))
         psum = ctx.enter_context(tc.psum_pool(name="psum", bufs=1))
 
-        def sb(name, width, dtype=F32):
-            return keep.tile([P, width], dtype, name=name, align_bytes=64)
+        def sb(name, width, dtype=F32, tag=""):
+            return keep.tile([P, width], dtype, name=name, tag=tag or name, align_bytes=64)
 
         def bank(name, tag):
             return psum.tile([P, S], F32, name=name, tag=tag)
@@ -48,7 +49,7 @@ def tile_picked_ypvcel_pow_p_kernel(
         word_win = [sb("word_win%d" % g, T, U32) for g in range(PASSES)]
         scale_win = sb("scale_win", T, U8)
         raw = {(w, g): sb("raw%d_%d" % (w, g), PACK * N) for w in (1, 2) for g in range(PASSES)}
-        rows = sb("rows", P)
+        rows = sb("rows", P, tag="stage0")
         ident = sb("ident", P)
 
         def load_words(g):
@@ -61,70 +62,74 @@ def tile_picked_ypvcel_pow_p_kernel(
             src = (w1 if w == 1 else w2)[g * P * PACK : (g + 1) * P * PACK, :]
             nc.sync.dma_start(out=raw[w, g][:], in_=src.rearrange("(p j) c -> p (j c)", j=PACK))
 
+        n_par = 2 * JB + HALVES
         nc.vector.memset(scale_win[:].bitcast(I32), 0)
         nc.gpsimd.memset(rows[:], 0.0)
         nc.sync.dma_start(offs_t[:], offs)
+        nc.sync.dma_start(mate_t[:], mate)
+        nc.sync.dma_start(out=rows[0:JB, :], in_=rser[0:1, :].rearrange("o (b p) -> (o b) p", p=P))
+        nc.sync.dma_start(out=rows[JB + HALVES : n_par, :], in_=gsh[0:1, :].rearrange("o (b p) -> (o b) p", p=P))
+        nc.sync.dma_start(out=rows[JB : JB + HALVES, :], in_=isat.rearrange("(h p) o -> (o h) p", p=P))
         load_words(0)
+        load_weight(2, 0)
         for q in range(4):
             nc.sync.dma_start(
                 out=scale_win[32 * q : 32 * q + 4 * PASSES, :].bitcast(I32),
                 in_=x_scales[:, 4 * q : 4 * q + 4, :].bitcast(I32),
             )
-        load_weight(2, 0)
-        load_words(1)
-        nc.sync.dma_start(out=rows[0:JB, :], in_=rser[0:1, :].rearrange("o (b p) -> (o b) p", p=P))
-        nc.sync.dma_start(out=rows[JB : 2 * JB, :], in_=gsh[0:1, :].rearrange("o (b p) -> (o b) p", p=P))
-        nc.sync.dma_start(out=rows[2 * JB : 2 * JB + HALVES, :], in_=isat.rearrange("(h p) o -> (o h) p", p=P))
-        load_weight(2, 1)
         load_weight(1, 0)
+        load_words(1)
+        load_weight(2, 1)
         load_weight(1, 1)
-        nc.sync.dma_start(mate_t[:], mate)
         make_identity(nc, ident[:])
 
         turned = bank("turned", "d0")
         nc.tensor.transpose(turned[:, 0:P], rows[:], ident[:])
+        logs = sb("logs", JB)
+        nc.scalar.activation(logs[:], turned[:, 0:JB], ACT.Ln, scale=1.3, bias=A_FLOOR)
+        ln_isat = [sb("ln_isat%d" % h, 1) for h in range(HALVES)]
+        for h in range(HALVES):
+            nc.scalar.activation(ln_isat[h][:], turned[:, JB + h : JB + h + 1], ACT.Ln, bias=LN_FLOOR)
         par = sb("par", 16)
-        nc.scalar.activation(par[:, 0:10], turned[:, 0:10], ACT.Copy)
-        r_c, g_c, isat_c = par[:, 0:JB], par[:, JB : 2 * JB], par[:, 2 * JB : 2 * JB + HALVES]
-        expo = sb("expo", HALVES * S + 8)
-        ac = sb("ac", 2 * JB)
-        rg = sb("rg", JB)
-        nc.gpsimd.tensor_scalar(ac[:, 0:JB], r_c, 1.3, LN_FLOOR, ALU.mult, ALU.max)
-        nc.gpsimd.tensor_tensor(rg[:], r_c, g_c, ALU.mult)
-        nc.gpsimd.tensor_scalar(ac[:, JB : 2 * JB], rg[:], 1.0, 1.0, ALU.mult, ALU.add)
-        inv = sb("inv", 2 * JB)
-        nc.vector.reciprocal(inv[:], ac[:])
-        inv_a, inv_c = inv[:, 0:JB], inv[:, JB : 2 * JB]
-        nc.gpsimd.tensor_tensor(expo[:, HALVES * S : HALVES * S + JB], ac[:, 0:JB], inv_c, ALU.mult)
-        nc.gpsimd.tensor_scalar(expo[:, HALVES * S + JB : HALVES * S + JB + HALVES], isat_c, 1.0, LN_FLOOR, ALU.mult, ALU.max)
-        ngc = sb("ngc", JB)
-        slope = sb("slope", JB)
-        level = sb("level", JB)
-        vk = sb("vk", JB)
-        r43 = sb("r43", JB)
-        kb = sb("kb", JB)
-        nc.gpsimd.tensor_tensor(ngc[:], g_c, inv_c, ALU.mult)
-        nc.gpsimd.tensor_scalar(slope[:], ngc[:], -0.75, 0.0, ALU.mult, ALU.add)
-        nc.gpsimd.tensor_scalar(vk[:], r_c, -0.3, -0.75, ALU.mult, ALU.add)
-        nc.gpsimd.tensor_tensor(level[:], ngc[:], vk[:], ALU.mult)
-        nc.gpsimd.tensor_scalar(r43[:], r_c, 1.0 / 0.75, 0.0, ALU.mult, ALU.add)
-        nc.gpsimd.tensor_scalar(kb[:], r_c, 0.4, 1.0, ALU.mult, ALU.add)
+        nc.scalar.activation(par[:, 0:n_par], turned[:, 0:n_par], ACT.Copy)
+        r_c, g_c = par[:, 0:JB], par[:, JB + HALVES : n_par]
+        a_c = sb("a_c", JB)
+        rgc1 = sb("rgc1", 2 * JB)
+        rg = rgc1[:, 0:JB]
+        nc.gpsimd.tensor_tensor(rg, r_c, g_c, ALU.mult)
+        nc.gpsimd.tensor_scalar(rgc1[:, JB : 2 * JB], rg, 1.0, 1.0, ALU.mult, ALU.add)
+        nc.gpsimd.tensor_scalar(a_c[:], r_c, 1.3, A_FLOOR, ALU.mult, ALU.add)
+        ln_rgc = sb("ln_rgc", 2 * JB)
+        nc.scalar.activation(ln_rgc[:], rgc1[:], ACT.Ln, bias=LN_FLOOR)
+        ln_c = ln_rgc[:, JB : 2 * JB]
+        inv_a = sb("inv_a", JB)
+        nc.vector.reciprocal(inv_a[:], a_c[:])
+        r03 = sb("r03", JB)
+        r15 = sb("r15", JB)
+        nc.gpsimd.tensor_scalar(r03[:], r_c, 0.39, 0.0, ALU.mult, ALU.add)
+        nc.gpsimd.tensor_scalar(r15[:], r_c, 1.0 / 1.5, 0.0, ALU.mult, ALU.add)
+        lac = sb("lac", JB)
+        lar = sb("lar", JB)
+        shift = sb("shift", JB)
+        nc.gpsimd.tensor_tensor(lar[:], logs[:, 0:JB], r03[:], ALU.add)
+        nc.gpsimd.tensor_tensor(lac[:], lar[:], ln_c, ALU.subtract)
+        nc.gpsimd.tensor_scalar(shift[:], lac[:], 1.0 / 1.95, 0.0, ALU.mult, ALU.add)
 
         words = [sb("words%d" % g, S, U32) for g in range(PASSES)]
         scales = sb("scales", S, U8)
         nc.vector.tensor_copy(words[0][:], word_win[0][:].indirect(offs_t[:]))
         nc.vector.tensor_copy(scales[:], scale_win[:].indirect(offs_t[:]))
-        nc.vector.tensor_copy(words[1][:], word_win[1][:].indirect(offs_t[:]))
 
         grouped = {}
         wq = {}
         ws = {}
 
-        def cast(w, g, h0, nh, copy):
-            t = sb("grouped%d_%d_%d" % (w, g, h0), nh * P * PACK, BF16)
+        def cast(w, g, h0, nh, copy, stage):
+            t = sb("grouped%d_%d_%d" % (w, g, h0), nh * P * PACK, BF16, tag="stage%d" % stage)
             grouped[w, g, h0] = t
-            src = raw[w, g][:].rearrange("p (j c) -> p c j", j=PACK)[:, h0 * P : (h0 + nh) * P, :]
-            copy(t[:].rearrange("p (c j) -> p c j", j=PACK), src)
+            run = P // 4
+            src = raw[w, g][:].rearrange("p (j c i) -> p c j i", j=PACK, i=4)[:, h0 * run : (h0 + nh) * run, :, :]
+            copy(t[:].rearrange("p (c i j) -> p c j i", j=PACK, i=4), src)
 
         def quantize(w, g, h0, nh):
             codes = sb("wq%d_%d_%d" % (w, g, h0), nh * P, U32)
@@ -148,20 +153,34 @@ def tile_picked_ypvcel_pow_p_kernel(
                     stop=(g == PASSES - 1 and b == JB - 1),
                 )
 
-        for g in range(PASSES):
-            cast(2, g, 0, HALVES, lambda o, i: nc.scalar.activation(o, i, ACT.Copy))
-            quantize(2, g, 0, HALVES)
+        def on_scalar(o, i):
+            nc.scalar.activation(o, i, ACT.Copy)
+
+        sig = [sb("sig0", S)]
+        for stage, w in enumerate((2, 1)):
+            cast(w, 0, 0, HALVES, on_scalar, stage)
+            quantize(w, 0, 0, HALVES)
             for h in range(HALVES):
-                product(2, g, h)
-        cast(1, 0, 0, HALVES, nc.vector.tensor_copy)
-        quantize(1, 0, 0, HALVES)
-        for h in range(HALVES):
-            product(1, 0, h)
-        for h in range(HALVES):
-            cast(1, 1, h, 1, nc.vector.tensor_copy)
-        for h in range(HALVES):
-            quantize(1, 1, h, 1)
-            product(1, 1, h)
+                product(w, 0, h)
+        inv_c_t = sb("inv_c", JB, tag="raw1_0")
+        nc.scalar.activation(inv_c_t[:], ln_rgc[:, 0:JB], ACT.Sigmoid, scale=-1.0)
+        inv_c = inv_c_t[:]
+        gc = sb("gc", JB)
+        slope = sb("slope", JB)
+        level = sb("level", JB)
+        rgc = sb("rgc", JB)
+        nc.gpsimd.tensor_tensor(gc[:], g_c, inv_c, ALU.mult)
+        nc.gpsimd.tensor_tensor(rgc[:], rg, inv_c, ALU.mult)
+        nc.gpsimd.tensor_scalar(slope[:], gc[:], -1.5, 0.0, ALU.mult, ALU.add)
+        nc.gpsimd.tensor_scalar(level[:], rgc[:], -0.3, 0.0, ALU.mult, ALU.add)
+        nc.vector.tensor_copy(words[1][:], word_win[1][:].indirect(offs_t[:]))
+        for w in (2, 1):
+            for h in range(HALVES):
+                cast(w, 1, h, 1, nc.vector.tensor_copy, h)
+            for h in range(HALVES):
+                quantize(w, 1, h, 1)
+                product(w, 1, h)
+        nc.scalar.activation(sig[0][:], y[2, 0][:], ACT.Sigmoid)
 
         def turn(dst, src, first, last):
             for b in range(JB):
@@ -175,82 +194,97 @@ def tile_picked_ypvcel_pow_p_kernel(
         def spread(col):
             return lambda b: col[:, b : b + 1].to_broadcast([P, P])
 
-        th = [sb("th%d" % h, S) for h in range(HALVES)]
+        down = sb("down", HALVES * S)
         for h in range(HALVES):
-            nc.scalar.activation(th[h][:], y[2, h][:], ACT.Tanh, scale=0.5)
-        for h in range(HALVES):
-            nc.scalar.activation(expo[:, h * S : (h + 1) * S], y[1, h][:], ACT.Exp)
-        capped = sb("capped", HALVES * S + 8)
-        n_ln = HALVES * S + JB + HALVES
-        nc.vector.tensor_scalar(capped[:, 0:n_ln], expo[:, 0:n_ln], LN_TOP, None, ALU.min)
+            nc.scalar.activation(down[:, h * S : (h + 1) * S], y[1, h][:], ACT.Sigmoid, scale=-1.0)
 
-        vsum = []
-        for h in range(HALVES):
-            th_t = bank("th_t%d" % h, "c%d" % h)
-            turn(th_t, blocks(th[h]), True, True)
-            volt = sb("volt%d" % h, S)
-            volt2 = sb("volt2_%d" % h, S)
-            nc.vector.tensor_scalar(volt[:], th_t[:], 0.75, 0.75, ALU.mult, ALU.add)
-            nc.vector.tensor_copy(volt2[:], volt[:])
-            vs = sb("vsum%d" % h, S)
-            for c0 in range(0, S, PIECE):
-                nc.vector.tensor_tensor(
-                    vs[:, c0 : c0 + PIECE],
-                    volt[:].indirect(mate_t[:, c0 // 16 : (c0 + PIECE) // 16]),
-                    volt2[:, c0 : c0 + PIECE],
-                    ALU.add,
-                )
-            vsum.append(vs)
+        volt = []
+        sig_t = []
+        vsum = [sb("vsum%d" % h, S) for h in range(HALVES)]
 
-        logs = sb("logs", 8)
-        nc.scalar.activation(logs[:, 0 : JB + HALVES], capped[:, HALVES * S : n_ln], ACT.Ln)
-        shift = sb("shift", JB)
-        nc.vector.scalar_tensor_tensor(shift[:], logs[:, 0:JB], 1.0 / 0.975, kb[:], ALU.mult, ALU.add)
-        soft_raw = [sb("soft_raw%d" % h, S) for h in range(HALVES)]
-        for h in range(HALVES):
-            nc.scalar.activation(soft_raw[h][:], capped[:, h * S : (h + 1) * S], ACT.Ln, bias=1.0)
+        def turn_sigmoid(h):
+            sig_t.append(bank("sig_t%d" % h, ("c0", "b0")[h]))
+            turn(sig_t[h], blocks(sig[h]), True, True)
+            volt.append(sb("volt%d" % h, S))
+
+        turn_sigmoid(0)
+        nc.vector.tensor_scalar(volt[0][:], sig_t[0][:], 1.5, None, ALU.mult)
+        volt2 = sb("volt2", S)
+        nc.vector.tensor_copy(volt2[:], volt[0][:])
+        for c0 in range(0, S, PIECE):
+            nc.vector.tensor_tensor(
+                vsum[0][:, c0 : c0 + PIECE],
+                volt[0][:].indirect(mate_t[:, c0 // 16 : (c0 + PIECE) // 16]),
+                volt2[:, c0 : c0 + PIECE],
+                ALU.add,
+            )
+
+        ln_down = sb("ln_down", HALVES * S)
+        for cols in (slice(0, S + LAP), slice(S + LAP, HALVES * S)):
+            nc.scalar.activation(ln_down[:, cols], down[:, cols], ACT.Ln, bias=LN_FLOOR)
+
+        sig.append(sb("sig1", S, tag="down"))
+        nc.scalar.activation(sig[1][:], y[2, 1][:], ACT.Sigmoid)
 
         u_t, w_t, x_t = [], [], []
         for h in range(HALVES):
-            u_t.append(bank("u_t%d" % h, "a%d" % h))
+            u_t.append(bank("u_t%d" % h, ("a0", "c0")[h]))
             w_t.append(bank("w_t%d" % h, "d%d" % h))
-            x_t.append(bank("x_t%d" % h, "c%d" % h))
+            x_t.append(bank("x_t%d" % h, ("c1", "b1")[h]))
             turn(w_t[h], spread(inv_a), True, False)
             turn(u_t[h], spread(shift), True, False)
         for h in range(HALVES):
             soft = sb("soft%d" % h, S)
             u = sb("u%d" % h, S)
             ngv = sb("ngv%d" % h, S)
-            nc.vector.tensor_tensor(soft[:], soft_raw[h][:], y[1, h][:], ALU.max)
+            nc.vector.scalar_tensor_tensor(soft[:], ln_down[:, h * S : (h + 1) * S], -1.0, y[1, h][:], ALU.mult, ALU.max)
+            if h == 0:
+                turn(x_t[h], blocks(soft), True, False)
             for b in range(JB):
                 nc.vector.scalar_tensor_tensor(
-                    u[:, blk(b)], soft[:, blk(b)], r43[:, b : b + 1], th[h][:, blk(b)], ALU.mult, ALU.add
+                    u[:, blk(b)], soft[:, blk(b)], r15[:, b : b + 1], sig[h][:, blk(b)], ALU.mult, ALU.add
                 )
             turn(u_t[h], blocks(u), False, True)
+            if h == 0:
+                turn_sigmoid(1)
             for b in range(JB):
                 nc.vector.tensor_scalar(
                     ngv[:, blk(b)], u[:, blk(b)], slope[:, b : b + 1], level[:, b : b + 1], ALU.mult, ALU.add
                 )
             turn(w_t[h], blocks(ngv), False, True)
-            turn(x_t[h], blocks(soft), True, False)
-            turn(x_t[h], blocks(ngv), False, True)
+            turn(x_t[h], blocks(ngv), h == 1, h == 0)
+            if h == 1:
+                turn(x_t[h], blocks(soft), False, True)
 
         cua = []
         for h in range(HALVES):
             gate = sb("gate%d" % h, S)
-            nc.scalar.activation(gate[:], u_t[h][:], ACT.Sigmoid, bias=logs[:, JB + h : JB + h + 1], scale=0.975)
+            nc.scalar.activation(gate[:], u_t[h][:], ACT.Sigmoid, bias=ln_isat[h][:], scale=1.95)
+            if h == 0:
+                nc.scalar.activation(volt[1][:], sig_t[1][:], ACT.Copy, scale=1.5)
             pull = sb("pull%d" % h, S)
             nc.vector.tensor_tensor(pull[:], gate[:], w_t[h][:], ALU.mult)
             c = sb("cua%d" % h, S)
             nc.vector.scalar_tensor_tensor(c[:], x_t[h][:], 0.3, pull[:], ALU.add, ALU.subtract)
             cua.append(c)
-        for h in range(HALVES):
+        volt_mate = sb("volt_mate", S)
+        for c0 in range(0, S, PIECE):
+            nc.scalar.activation(
+                volt_mate[:, c0 : c0 + PIECE], volt[1][:].indirect(mate_t[:, c0 // 16 : (c0 + PIECE) // 16]), ACT.Copy
+            )
+        nc.vector.scalar_tensor_tensor(vsum[1][:], sig_t[1][:], 1.5, volt_mate[:], ALU.mult, ALU.add)
+        for h, width in ((0, S), (1, PIECE)):
+            other = sb("other%d" % h, S)
             for c0 in range(0, S, PIECE):
-                cols = slice(c0, c0 + PIECE)
-                other = sb("other%d_%d" % (h, c0), PIECE)
-                nc.scalar.activation(other[:], cua[h][:].indirect(mate_t[:, c0 // 16 : (c0 + PIECE) // 16]), ACT.Copy)
-                least = sb("least%d_%d" % (h, c0), PIECE)
-                nc.vector.tensor_tensor(least[:], other[:], cua[h][:, cols], ALU.min)
-                res = sb("res%d_%d" % (h, c0), PIECE)
-                nc.vector.tensor_tensor(res[:], least[:], vsum[h][:, cols], ALU.mult)
-                nc.sync.dma_start(out=out[blk(h), cols], in_=res[:])
+                nc.scalar.activation(
+                    other[:, c0 : c0 + PIECE], cua[h][:].indirect(mate_t[:, c0 // 16 : (c0 + PIECE) // 16]), ACT.Copy
+                )
+            least = sb("least%d" % h, S)
+            res = sb("res%d" % h, S)
+            for c0 in range(0, S, width):
+                cols = slice(c0, c0 + width)
+                nc.vector.tensor_tensor(least[:, cols], other[:, cols], cua[h][:, cols], ALU.min)
+            for c0 in range(0, S, width):
+                cols = slice(c0, c0 + width)
+                nc.vector.tensor_tensor(res[:, cols], least[:, cols], vsum[h][:, cols], ALU.mult)
+                nc.sync.dma_start(out=out[blk(h), cols], in_=res[:, cols])

@@ -274,7 +274,7 @@ def tile_picked_ypvcel_pow_p_kernel(
             )
         nc.vector.scalar_tensor_tensor(vsum[1][:], sig_t[1][:], 1.5, volt_mate[:], ALU.mult, ALU.add)
         for h, width in ((0, S), (1, PIECE)):
-            other = sb("other%d" % h, S)
+            other = sb("other%d" % h, S, tag=("ln_isat1", "other1")[h])
             for c0 in range(0, S, PIECE):
                 nc.scalar.activation(
                     other[:, c0 : c0 + PIECE], cua[h][:].indirect(mate_t[:, c0 // 16 : (c0 + PIECE) // 16]), ACT.Copy

@@ -156,7 +156,6 @@ def tile_picked_ypvcel_pow_p_kernel(
         def on_scalar(o, i):
             nc.scalar.activation(o, i, ACT.Copy)
 
-        sig = [sb("sig0", S)]
         for stage, w in enumerate((2, 1)):
             cast(w, 0, 0, HALVES, on_scalar, stage)
             quantize(w, 0, 0, HALVES)
@@ -174,12 +173,16 @@ def tile_picked_ypvcel_pow_p_kernel(
         nc.gpsimd.tensor_scalar(slope[:], gc[:], -1.5, 0.0, ALU.mult, ALU.add)
         nc.gpsimd.tensor_scalar(level[:], rgc[:], -0.3, 0.0, ALU.mult, ALU.add)
         nc.vector.tensor_copy(words[1][:], word_win[1][:].indirect(offs_t[:]))
-        for w in (2, 1):
-            for h in range(HALVES):
-                cast(w, 1, h, 1, nc.vector.tensor_copy, h)
-            for h in range(HALVES):
-                quantize(w, 1, h, 1)
-                product(w, 1, h)
+        for w, h, copy, stage in (
+            (2, 0, nc.vector.tensor_copy, 0),
+            (1, 0, nc.vector.tensor_copy, 0),
+            (1, 1, on_scalar, 1),
+            (2, 1, nc.vector.tensor_copy, 0),
+        ):
+            cast(w, 1, h, 1, copy, stage)
+            quantize(w, 1, h, 1)
+            product(w, 1, h)
+        sig = [sb("sig0", S, tag="raw1_1")]
         nc.scalar.activation(sig[0][:], y[2, 0][:], ACT.Sigmoid)
 
         def turn(dst, src, first, last):
@@ -272,14 +275,14 @@ def tile_picked_ypvcel_pow_p_kernel(
             nc.scalar.activation(
                 volt_mate[:, c0 : c0 + PIECE], volt[1][:].indirect(mate_t[:, c0 // 16 : (c0 + PIECE) // 16]), ACT.Copy
             )
-        nc.vector.scalar_tensor_tensor(vsum[1][:], sig_t[1][:], 1.5, volt_mate[:], ALU.mult, ALU.add)
+        nc.gpsimd.tensor_tensor(vsum[1][:], volt[1][:], volt_mate[:], ALU.add)
         for h, width in ((0, S), (1, PIECE)):
             other = sb("other%d" % h, S, tag=("ln_isat1", "other1")[h])
             for c0 in range(0, S, PIECE):
                 nc.scalar.activation(
                     other[:, c0 : c0 + PIECE], cua[h][:].indirect(mate_t[:, c0 // 16 : (c0 + PIECE) // 16]), ACT.Copy
                 )
-            least = sb("least%d" % h, S)
+            least = sb("least%d" % h, S, tag=("pull1", "least1")[h])
             res = sb("res%d" % h, S)
             for c0 in range(0, S, width):
                 cols = slice(c0, c0 + width)

from contextlib import ExitStack

import concourse.mybir as mybir
from concourse.masks import make_identity

K, T, S, N = 1024, 1024, 512, 256
FLOPS = 2 * 2 * K * N * S

F32 = mybir.dt.float32
BF16 = mybir.dt.bfloat16
U32 = mybir.dt.uint32
I32 = mybir.dt.int32
U16 = mybir.dt.uint16
U8 = mybir.dt.uint8
FP8X4 = mybir.dt.float8_e4m3fn_x4
ALU = mybir.AluOpType
ACT = mybir.ActivationFunctionType

P = 128
PACK = 4
PASSES = K // (P * PACK)
JB = S // P
HALVES = N // P
PIECE = 256
LN_FLOOR = 2.0 ** -60
A_FLOOR = 2.0 ** -50
LAP = 16


def tile_picked_ypvcel_pow_p_kernel(
    tc, x_words, x_scales, w1, w2, rser, isat, gsh, offs, mate, out
):
    nc = tc.nc
    with ExitStack() as ctx:
        keep = ctx.enter_context(tc.tile_pool(name="keep", bufs=1))
        psum = ctx.enter_context(tc.psum_pool(name="psum", bufs=1))

        def sb(name, width, dtype=F32, tag=""):
            return keep.tile([P, width], dtype, name=name, tag=tag or name, align_bytes=64)

        def bank(name, tag):
            return psum.tile([P, S], F32, name=name, tag=tag)

        def blk(b):
            return slice(b * P, (b + 1) * P)

        offs_t = keep.tile([P, S // 16], U16, name="offs_t")
        mate_t = keep.tile([P, S // 16], U16, name="mate_t")
        word_win = [sb("word_win%d" % g, T, U32) for g in range(PASSES)]
        scale_win = sb("scale_win", T, U8)
        raw = {(w, g): sb("raw%d_%d" % (w, g), PACK * N) for w in (1, 2) for g in range(PASSES)}
        rows = sb("rows", P, tag="stage0")
        ident = sb("ident", P)

        def load_words(g):
            nc.sync.dma_start(
                out=word_win[g][:].bitcast(I32),
                in_=x_words[g].rearrange("p n t -> p (n t)").bitcast(I32),
            )

        def load_weight(w, g):
            src = (w1 if w == 1 else w2)[g * P * PACK : (g + 1) * P * PACK, :]
            nc.sync.dma_start(out=raw[w, g][:], in_=src.rearrange("(p j) c -> p (j c)", j=PACK))

        n_par = 2 * JB + HALVES
        nc.vector.memset(scale_win[:].bitcast(I32), 0)
        nc.gpsimd.memset(rows[:], 0.0)
        nc.sync.dma_start(offs_t[:], offs)
        nc.sync.dma_start(mate_t[:], mate)
        nc.sync.dma_start(out=rows[0:JB, :], in_=rser[0:1, :].rearrange("o (b p) -> (o b) p", p=P))
        nc.sync.dma_start(out=rows[JB + HALVES : n_par, :], in_=gsh[0:1, :].rearrange("o (b p) -> (o b) p", p=P))
        nc.sync.dma_start(out=rows[JB : JB + HALVES, :], in_=isat.rearrange("(h p) o -> (o h) p", p=P))
        load_words(0)
        load_weight(2, 0)
        for q in range(4):
            nc.sync.dma_start(
                out=scale_win[32 * q : 32 * q + 4 * PASSES, :].bitcast(I32),
                in_=x_scales[:, 4 * q : 4 * q + 4, :].bitcast(I32),
            )
        load_weight(1, 0)
        load_words(1)
        load_weight(2, 1)
        load_weight(1, 1)
        make_identity(nc, ident[:])

        turned = bank("turned", "d0")
        nc.tensor.transpose(turned[:, 0:P], rows[:], ident[:])
        logs = sb("logs", JB)
        nc.scalar.activation(logs[:], turned[:, 0:JB], ACT.Ln, scale=1.3, bias=A_FLOOR)
        ln_isat = [sb("ln_isat%d" % h, 1) for h in range(HALVES)]
        for h in range(HALVES):
            nc.scalar.activation(ln_isat[h][:], turned[:, JB + h : JB + h + 1], ACT.Ln, bias=LN_FLOOR)
        par = sb("par", 16)
        nc.scalar.activation(par[:, 0:n_par], turned[:, 0:n_par], ACT.Copy)
        r_c, g_c = par[:, 0:JB], par[:, JB + HALVES : n_par]
        a_c = sb("a_c", JB)
        rgc1 = sb("rgc1", 2 * JB)
        rg = rgc1[:, 0:JB]
        nc.gpsimd.tensor_tensor(rg, r_c, g_c, ALU.mult)
        nc.gpsimd.tensor_scalar(rgc1[:, JB : 2 * JB], rg, 1.0, 1.0, ALU.mult, ALU.add)
        nc.gpsimd.tensor_scalar(a_c[:], r_c, 1.3, A_FLOOR, ALU.mult, ALU.add)
        ln_rgc = sb("ln_rgc", 2 * JB)
        nc.scalar.activation(ln_rgc[:], rgc1[:], ACT.Ln, bias=LN_FLOOR)
        ln_c = ln_rgc[:, JB : 2 * JB]
        inv_a = sb("inv_a", JB)
        nc.vector.reciprocal(inv_a[:], a_c[:])
        r03 = sb("r03", JB)
        r15 = sb("r15", JB)
        nc.gpsimd.tensor_scalar(r03[:], r_c, 0.39, 0.0, ALU.mult, ALU.add)
        nc.gpsimd.tensor_scalar(r15[:], r_c, 1.0 / 1.5, 0.0, ALU.mult, ALU.add)
        lac = sb("lac", JB)
        lar = sb("lar", JB)
        shift = sb("shift", JB)
        nc.gpsimd.tensor_tensor(lar[:], logs[:, 0:JB], r03[:], ALU.add)
        nc.gpsimd.tensor_tensor(lac[:], lar[:], ln_c, ALU.subtract)
        nc.gpsimd.tensor_scalar(shift[:], lac[:], 1.0 / 1.95, 0.0, ALU.mult, ALU.add)

        words = [sb("words%d" % g, S, U32) for g in range(PASSES)]
        scales = sb("scales", S, U8)
        nc.vector.tensor_copy(words[0][:], word_win[0][:].indirect(offs_t[:]))
        nc.vector.tensor_copy(scales[:], scale_win[:].indirect(offs_t[:]))

        grouped = {}
        wq = {}
        ws = {}

        def cast(w, g, h0, nh, copy, stage):
            t = sb("grouped%d_%d_%d" % (w, g, h0), nh * P * PACK, BF16, tag="stage%d" % stage)
            grouped[w, g, h0] = t
            run = P // 4
            src = raw[w, g][:].rearrange("p (j c i) -> p c j i", j=PACK, i=4)[:, h0 * run : (h0 + nh) * run, :, :]
            copy(t[:].rearrange("p (c i j) -> p c j i", j=PACK, i=4), src)

        def quantize(w, g, h0, nh):
            codes = sb("wq%d_%d_%d" % (w, g, h0), nh * P, U32)
            plane = sb("ws%d_%d_%d" % (w, g, h0), nh * P, U8)
            nc.vector.quantize_mx(codes[:].bitcast(FP8X4), plane[:], grouped[w, g, h0][:])
            for h in range(nh):
                wq[w, g, h0 + h] = codes[:, blk(h)]
                ws[w, g, h0 + h] = plane[:, blk(h)]

        y = {(w, h): bank("y%d_%d" % (w, h), ("a%d" if w == 2 else "b%d") % h) for w in (1, 2) for h in range(HALVES)}

        def product(w, g, h):
            for b in range(JB):
                nc.tensor.matmul_mx(
                    out=y[w, h][:, blk(b)],
                    lhsT=words[g][:, blk(b)].bitcast(FP8X4),
                    lhsT_scale=scales[4 * g : P, blk(b)],
                    rhs=wq[w, g, h].bitcast(FP8X4),
                    rhs_scale=ws[w, g, h],
                    start=(g == 0 and b == 0),
                    stop=(g == PASSES - 1 and b == JB - 1),
                )

        def on_scalar(o, i):
            nc.scalar.activation(o, i, ACT.Copy)

        for stage, w in enumerate((2, 1)):
            cast(w, 0, 0, HALVES, on_scalar, stage)
            quantize(w, 0, 0, HALVES)
            for h in range(HALVES):
                product(w, 0, h)
        inv_c_t = sb("inv_c", JB, tag="raw1_0")
        nc.scalar.activation(inv_c_t[:], ln_rgc[:, 0:JB], ACT.Sigmoid, scale=-1.0)
        inv_c = inv_c_t[:]
        gc = sb("gc", JB)
        slope = sb("slope", JB)
        level = sb("level", JB)
        rgc = sb("rgc", JB)
        nc.gpsimd.tensor_tensor(gc[:], g_c, inv_c, ALU.mult)
        nc.gpsimd.tensor_tensor(rgc[:], rg, inv_c, ALU.mult)
        nc.gpsimd.tensor_scalar(slope[:], gc[:], -1.5, 0.0, ALU.mult, ALU.add)
        nc.gpsimd.tensor_scalar(level[:], rgc[:], -0.3, 0.0, ALU.mult, ALU.add)
        nc.vector.tensor_copy(words[1][:], word_win[1][:].indirect(offs_t[:]))
        for w, h, copy, stage in (
            (2, 0, nc.vector.tensor_copy, 0),
            (1, 0, nc.vector.tensor_copy, 0),
            (1, 1, on_scalar, 1),
            (2, 1, nc.vector.tensor_copy, 0),
        ):
            cast(w, 1, h, 1, copy, stage)
            quantize(w, 1, h, 1)
            product(w, 1, h)
        sig = [sb("sig0", S, tag="raw1_1")]
        nc.scalar.activation(sig[0][:], y[2, 0][:], ACT.Sigmoid)

        def turn(dst, src, first, last):
            for b in range(JB):
                nc.tensor.matmul(
                    dst[:, blk(b)], src(b), ident[:], start=(first and b == 0), stop=(last and b == JB - 1), is_transpose=True
                )

        def blocks(t):
            return lambda b: t[:, blk(b)]

        def spread(col):
            return lambda b: col[:, b : b + 1].to_broadcast([P, P])

        down = sb("down", HALVES * S)
        for h in range(HALVES):
            nc.scalar.activation(down[:, h * S : (h + 1) * S], y[1, h][:], ACT.Sigmoid, scale=-1.0)

        volt = []
        sig_t = []
        vsum = [sb("vsum%d" % h, S) for h in range(HALVES)]

        def turn_sigmoid(h):
            sig_t.append(bank("sig_t%d" % h, ("c0", "b0")[h]))
            turn(sig_t[h], blocks(sig[h]), True, True)
            volt.append(sb("volt%d" % h, S))

        turn_sigmoid(0)
        nc.vector.tensor_scalar(volt[0][:], sig_t[0][:], 1.5, None, ALU.mult)
        volt2 = sb("volt2", S)
        nc.vector.tensor_copy(volt2[:], volt[0][:])
        for c0 in range(0, S, PIECE):
            nc.vector.tensor_tensor(
                vsum[0][:, c0 : c0 + PIECE],
                volt[0][:].indirect(mate_t[:, c0 // 16 : (c0 + PIECE) // 16]),
                volt2[:, c0 : c0 + PIECE],
                ALU.add,
            )

        ln_down = sb("ln_down", HALVES * S)
        for cols in (slice(0, S + LAP), slice(S + LAP, HALVES * S)):
            nc.scalar.activation(ln_down[:, cols], down[:, cols], ACT.Ln, bias=LN_FLOOR)

        sig.append(sb("sig1", S, tag="down"))
        nc.scalar.activation(sig[1][:], y[2, 1][:], ACT.Sigmoid)

        u_t, w_t, x_t = [], [], []
        for h in range(HALVES):
            u_t.append(bank("u_t%d" % h, ("a0", "c0")[h]))
            w_t.append(bank("w_t%d" % h, "d%d" % h))
            x_t.append(bank("x_t%d" % h, ("c1", "b1")[h]))
            turn(w_t[h], spread(inv_a), True, False)
            turn(u_t[h], spread(shift), True, False)
        for h in range(HALVES):
            soft = sb("soft%d" % h, S)
            u = sb("u%d" % h, S)
            ngv = sb("ngv%d" % h, S)
            nc.vector.scalar_tensor_tensor(soft[:], ln_down[:, h * S : (h + 1) * S], -1.0, y[1, h][:], ALU.mult, ALU.max)
            if h == 0:
                turn(x_t[h], blocks(soft), True, False)
            for b in range(JB):
                nc.vector.scalar_tensor_tensor(
                    u[:, blk(b)], soft[:, blk(b)], r15[:, b : b + 1], sig[h][:, blk(b)], ALU.mult, ALU.add
                )
            turn(u_t[h], blocks(u), False, True)
            if h == 0:
                turn_sigmoid(1)
            for b in range(JB):
                nc.vector.tensor_scalar(
                    ngv[:, blk(b)], u[:, blk(b)], slope[:, b : b + 1], level[:, b : b + 1], ALU.mult, ALU.add
                )
            turn(w_t[h], blocks(ngv), False, True)
            turn(x_t[h], blocks(ngv), h == 1, h == 0)
            if h == 1:
                turn(x_t[h], blocks(soft), False, True)

        cua = []
        for h in range(HALVES):
            gate = sb("gate%d" % h, S)
            nc.scalar.activation(gate[:], u_t[h][:], ACT.Sigmoid, bias=ln_isat[h][:], scale=1.95)
            if h == 0:
                nc.scalar.activation(volt[1][:], sig_t[1][:], ACT.Copy, scale=1.5)
            pull = sb("pull%d" % h, S)
            nc.vector.tensor_tensor(pull[:], gate[:], w_t[h][:], ALU.mult)
            c = sb("cua%d" % h, S)
            nc.vector.scalar_tensor_tensor(c[:], x_t[h][:], 0.3, pull[:], ALU.add, ALU.subtract)
            cua.append(c)
        volt_mate = sb("volt_mate", S)
        for c0 in range(0, S, PIECE):
            nc.scalar.activation(
                volt_mate[:, c0 : c0 + PIECE], volt[1][:].indirect(mate_t[:, c0 // 16 : (c0 + PIECE) // 16]), ACT.Copy
            )
        nc.gpsimd.tensor_tensor(vsum[1][:], volt[1][:], volt_mate[:], ALU.add)
        for h, width in ((0, S), (1, PIECE)):
            other = sb("other%d" % h, S, tag=("ln_isat1", "other1")[h])
            for c0 in range(0, S, PIECE):
                nc.scalar.activation(
                    other[:, c0 : c0 + PIECE], cua[h][:].indirect(mate_t[:, c0 // 16 : (c0 + PIECE) // 16]), ACT.Copy
                )
            least = sb("least%d" % h, S, tag=("pull1", "least1")[h])
            res = sb("res%d" % h, S)
            for c0 in range(0, S, width):
                cols = slice(c0, c0 + width)
                nc.vector.tensor_tensor(least[:, cols], other[:, cols], cua[h][:, cols], ALU.min)
            for c0 in range(0, S, width):
                cols = slice(c0, c0 + width)
                nc.vector.tensor_tensor(res[:, cols], least[:, cols], vsum[h][:, cols], ALU.mult)
                nc.sync.dma_start(out=out[blk(h), cols], in_=res[:, cols])
